import numpy as np
import ml_dtypes


def mxq(x, axis, fmt="e4m3"):
    dtype, down = {"e4m3": (ml_dtypes.float8_e4m3fn, 7), "e5m2": (ml_dtypes.float8_e5m2, 14)}[fmt]
    v = np.moveaxis(np.asarray(x, np.float32).astype(ml_dtypes.bfloat16).astype(np.float64), axis, -1)
    blocks = v.reshape(v.shape[:-1] + (-1, 32))
    amax = np.abs(blocks).max(-1, keepdims=True)
    byte = np.maximum(np.where(amax > 0, np.frexp(amax)[1] - 1 + 127, 0) - down, 1)
    scale = np.exp2(byte - 127.0)
    codes = (blocks / scale).astype(np.float32).astype(dtype).astype(np.float64)
    return np.moveaxis((codes * scale).reshape(v.shape), -1, axis)


WIDE = False


def mx_kscale(k):
    if not WIDE:
        return np.ones(k)
    levels = np.array([30, -30])
    if k % 512:
        return np.exp2(np.random.permutation(np.resize(levels, k // 32))).repeat(32)
    a = np.empty((k // 512, 16))
    for p in range(k // 512):
        a[p, :8] = np.random.permutation(np.resize(levels, 8))
        for g in range(8):
            far = levels[np.abs(levels - a[p, g]) >= 10]
            a[p, g + 8] = far[np.random.randint(len(far))]
    return np.exp2(a.ravel()).repeat(32)


def f64(x):
    return np.asarray(x).astype(np.float64)


def striped(idx):
    return np.tile(np.asarray(idx).reshape(-1, 16).T, (8, 1)).astype(np.uint16)


def unstriped(offs):
    return offs[:16].T.reshape(-1).astype(np.int64)


E2M1 = np.array([0.0, 0.5, 1.0, 1.5, 2.0, 3.0, 4.0, 6.0, -0.0, -0.5, -1.0, -1.5, -2.0, -3.0, -4.0, -6.0])


def pack_weight(w, fmt):
    k, n = w.shape
    w = f64(np.asarray(w, np.float32).astype(ml_dtypes.bfloat16)).reshape(k // 32, 32, n)
    amax = np.abs(w).max(1)
    if fmt in ("e4m3", "e5m2"):
        byte = np.frexp(amax)[1] - 1 + 127 - (7 if fmt == "e4m3" else 14)
    else:
        mant, ex = np.frexp(amax / 6.0)
        byte = np.where(mant > 0.5, ex, ex - 1) + 127
    byte = np.clip(np.where(amax > 0, byte, 1), 1, 254)
    scaled = (w * np.exp2(127.0 - byte)[:, None, :]).reshape(k, n).astype(np.float32)
    by_word = np.ascontiguousarray(scaled.reshape(k // 512, 128, 4, n).transpose(0, 1, 3, 2))
    if fmt in ("e4m3", "e5m2"):
        words = by_word.astype(ml_dtypes.float8_e4m3fn if fmt == "e4m3" else ml_dtypes.float8_e5m2).view(np.uint8)
    else:
        c = by_word.astype(ml_dtypes.float4_e2m1fn).view(np.uint8) & 0xF
        words = (c[..., 0::2] | (c[..., 1::2] << 4)).reshape(k // 512, 128, 2 * n)
    return np.ascontiguousarray(words), np.ascontiguousarray(byte.astype(np.uint8).reshape(k // 512, 16, n))


def unpack_weight(words, scales, fmt):
    g, _, n = scales.shape
    words = np.ascontiguousarray(words).reshape(g, 128, n, -1)
    if fmt in ("e4m3", "e5m2"):
        vals = words.view(ml_dtypes.float8_e4m3fn if fmt == "e4m3" else ml_dtypes.float8_e5m2).astype(np.float64)
    else:
        nib = np.empty((g, 128, n, 4), np.uint8)
        nib[..., 0::2] = words & 0xF
        nib[..., 1::2] = words >> 4
        vals = E2M1[nib]
    vals = vals * np.repeat(np.exp2(scales.astype(np.float64) - 127.0), 8, axis=1)[..., None]
    return vals.transpose(0, 1, 3, 2).reshape(g * 512, n)


def sigmoid(v):
    return 1.0 / (1.0 + np.exp(-v))


K, F, T, Z, J, R, N, O = 512, 512, 1024, 1024, 256, 512, 256, 128


def setup_inputs():
    n = np.random.standard_normal
    idx = np.random.permutation(T)[:J]
    idx2 = np.random.permutation(Z)[:J]
    idx3 = np.random.permutation(J)[:O]
    idx4 = np.random.permutation(J)[:O]
    idx5 = np.random.permutation(J)[:O]
    fk = mx_kscale(K)
    fr = mx_kscale(R)
    ff = mx_kscale(F)
    xtp = pack_weight(n((K, T)) / fk[:, None], "e5m2")
    wp = pack_weight(n((K, R)) * 1 / np.sqrt(K) * fk[:, None] * fr, "e2m1")
    xop = pack_weight(n((F, Z)) / ff[:, None], "e4m3")
    w0p = pack_weight(n((F, R)) * 1 / np.sqrt(F) * ff[:, None] * fr, "e2m1")
    wbp = pack_weight(n((R, N)) * 1 / np.sqrt(R) / fr[:, None], "e2m1")
    wcp = pack_weight(n((R, N)) * 1 / np.sqrt(R) / fr[:, None], "e4m3")
    wdp = pack_weight(n((R, N)) * 1 / np.sqrt(R) / fr[:, None], "e5m2")
    return {
        "xt_words": xtp[0],
        "xt_scales": xtp[1],
        "w_words": wp[0],
        "w_scales": wp[1],
        "xo_words": xop[0],
        "xo_scales": xop[1],
        "w0_words": w0p[0],
        "w0_scales": w0p[1],
        "wb_words": wbp[0],
        "wb_scales": wbp[1],
        "wc_words": wcp[0],
        "wc_scales": wcp[1],
        "wd_words": wdp[0],
        "wd_scales": wdp[1],
        "so": (np.random.uniform(0.6, 1.6, (N, 1))).astype(np.float32),
        "bo": (np.random.uniform(-1.0, 1.0, (N, 1))).astype(np.float32),
        "offs": striped(idx),
        "offs2": striped(idx2),
        "offs3": striped(idx3),
        "offs4": striped(idx4),
        "offs5": striped(idx5),
    }


def reference(xt_words, xt_scales, w_words, w_scales, xo_words, xo_scales, w0_words, w0_scales, wb_words, wb_scales, wc_words, wc_scales, wd_words, wd_scales, so, bo, offs, offs2, offs3, offs4, offs5):
    idx = unstriped(offs)
    idx2 = unstriped(offs2)
    idx3 = unstriped(offs3)
    idx4 = unstriped(offs4)
    idx5 = unstriped(offs5)
    xtu = unpack_weight(xt_words, xt_scales, "e5m2")
    wu = unpack_weight(w_words, w_scales, "e2m1")
    xou = unpack_weight(xo_words, xo_scales, "e4m3")
    w0u = unpack_weight(w0_words, w0_scales, "e2m1")
    wbu = unpack_weight(wb_words, wb_scales, "e2m1")
    wcu = unpack_weight(wc_words, wc_scales, "e4m3")
    wdu = unpack_weight(wd_words, wd_scales, "e5m2")
    xtidxg = xtu[:, idx]
    xoidx2g = xou[:, idx2]
    a = wu.T @ xtidxg + w0u.T @ xoidx2g
    hid = np.maximum(a, 0.0)
    hidq = mxq(hid, 0, "e4m3")
    p = wbu.T @ hidq
    q = wcu.T @ hidq
    m0 = wdu.T @ hidq
    y = np.maximum(p[:, idx3], q[:, idx4]) * sigmoid(m0[:, idx5] * f64(so) + f64(bo))
    return y

@@ -1,0 +1,190 @@
+from contextlib import ExitStack
+
+import concourse.mybir as mybir
+
+K, T, J, R, N, O = 512, 1024, 256, 512, 256, 128
+FLOPS = 2 * 2 * K * R * J + 3 * 2 * R * N * J
+
+F32 = mybir.dt.float32
+BF16 = mybir.dt.bfloat16
+I32 = mybir.dt.int32
+U32 = mybir.dt.uint32
+U16 = mybir.dt.uint16
+U8 = mybir.dt.uint8
+E4M3 = mybir.dt.float8_e4m3fn_x4
+E5M2 = mybir.dt.float8_e5m2_x4
+E2M1 = mybir.dt.float4_e2m1fn_x4
+ACT = mybir.ActivationFunctionType
+ALU = mybir.AluOpType
+
+P = 128
+ROWS = 16
+HALF = 128
+
+
+def tile_list_threeoutcomes_bank_kernel(
+    tc, xt_words, xt_scales, w_words, w_scales, xo_words, xo_scales, w0_words, w0_scales,
+    wb_words, wb_scales, wc_words, wc_scales, wd_words, wd_scales, so, bo,
+    offs, offs2, offs3, offs4, offs5, out,
+):
+    nc = tc.nc
+    with ExitStack() as ctx:
+        pool = ctx.enter_context(tc.tile_pool(name="sbuf", bufs=1))
+        psum = ctx.enter_context(tc.psum_pool(name="psum", bufs=1))
+
+        def sb(name, shape, dtype, tag=""):
+            return pool.tile(shape, dtype, name=name, tag=tag or name, align_bytes=64)
+
+        def words(ap):
+            return ap[0].rearrange("p n t -> p (n t)").bitcast(I32)
+
+        def per_block(scales):
+            rows = scales[0].bitcast(I32)
+            return rows.unsqueeze(1).broadcast_to([ROWS, 8, rows.shape[1]])
+
+        def gather_rows(planes):
+            for r in range(1, 4):
+                nc.sync.dma_start(
+                    out=planes[r:P:32, :].bitcast(I32),
+                    in_=planes[8 * r : P : 32, :].bitcast(I32),
+                )
+
+        xt_tab = sb("xt_tab", [P, T], I32)
+        xo_tab = sb("xo_tab", [P, T], I32)
+        planes2 = sb("planes2", [P, 3 * N], U8)
+        nc.gpsimd.dma_start(out=xt_tab[:], in_=words(xt_words))
+        nc.gpsimd.dma_start(out=xo_tab[:], in_=words(xo_words))
+        for i, sc in enumerate((wd_scales, wb_scales, wc_scales)):
+            nc.gpsimd.dma_start(out=planes2[:, i * N : (i + 1) * N].bitcast(I32), in_=per_block(sc))
+
+        l1 = sb("l1", [P, J // 16], U16)
+        l2 = sb("l2", [P, J // 16], U16)
+        l3 = sb("l3", [P, O // 16], U16)
+        l4 = sb("l4", [P, O // 16], U16)
+        l5 = sb("l5", [P, O // 16], U16)
+        xt_rows = sb("xt_rows", [P, T], U8)
+        xo_rows = sb("xo_rows", [P, T], U8)
+        w_rows = sb("w_rows", [P, R], U8)
+        w0_rows = sb("w0_rows", [P, R], U8)
+        w_raw = sb("w_raw", [P, 2 * R], U8)
+        w0_raw = sb("w0_raw", [P, 2 * R], U8)
+        nc.sync.dma_start(out=xt_rows[:].bitcast(I32), in_=per_block(xt_scales))
+        nc.sync.dma_start(l1[:], offs)
+        nc.sync.dma_start(out=w_rows[:].bitcast(I32), in_=per_block(w_scales))
+        nc.sync.dma_start(out=xo_rows[:].bitcast(I32), in_=per_block(xo_scales))
+        nc.sync.dma_start(l2[:], offs2)
+        nc.sync.dma_start(out=w0_rows[:].bitcast(I32), in_=per_block(w0_scales))
+        nc.sync.dma_start(out=w_raw[:].bitcast(I32), in_=w_words[0].bitcast(I32))
+        nc.sync.dma_start(out=w0_raw[:].bitcast(I32), in_=w0_words[0].bitcast(I32))
+        nc.sync.dma_start(l5[:], offs5)
+        nc.sync.dma_start(l3[:], offs3)
+        nc.sync.dma_start(l4[:], offs4)
+
+        planes1 = []
+        for i, (x_rows, lst, wt_rows) in enumerate(((xt_rows, l1, w_rows), (xo_rows, l2, w0_rows))):
+            picked = sb("picked%d" % i, [P, J], U8)
+            planes = sb("planes1_%d" % i, [P, J + R], U8)
+            nc.vector.tensor_copy(picked[:], x_rows[:].indirect(lst[:]))
+            nc.vector.tensor_copy(
+                planes[:, J:].rearrange("p (t m) -> p t m", t=4),
+                wt_rows[:].rearrange("p (m t) -> p t m", t=4),
+            )
+            nc.vector.tensor_copy(planes[:, 0:J].bitcast(I32), picked[:].bitcast(I32))
+            gather_rows(planes)
+            planes1.append(planes)
+
+        x_g = []
+        w_dealt = []
+        for i, (tab, lst, raw) in enumerate(((xt_tab, l1, w_raw), (xo_tab, l2, w0_raw))):
+            g = sb("x_g%d" % i, [P, J], U32)
+            dealt = sb("w_dealt%d" % i, [P, 2 * R], U8)
+            nc.vector.tensor_copy(g[:], tab[:].bitcast(U32).indirect(lst[:]))
+            nc.vector.tensor_copy(
+                dealt[:].bitcast(U16).rearrange("p (t m) -> p t m", t=4),
+                raw[:].bitcast(U16).rearrange("p (m t) -> p t m", t=4),
+            )
+            x_g.append(g)
+            w_dealt.append(dealt)
+
+        w2 = sb("w2", [P, 10 * N], U8, tag="xt_tab")
+        wd_sb = w2[:, 0 : 4 * N].bitcast(I32)
+        wb_sb = w2[:, 4 * N : 6 * N]
+        wc_sb = w2[:, 6 * N : 10 * N].bitcast(I32)
+        nc.sync.dma_start(out=wd_sb, in_=words(wd_words))
+        nc.sync.dma_start(out=wb_sb.bitcast(I32), in_=wb_words[0].bitcast(I32))
+        nc.sync.dma_start(out=wc_sb, in_=words(wc_words))
+        gather_rows(planes2)
+
+        cal = sb("cal", [P, 16], F32, tag="xo_tab")
+        with nc.allow_non_contiguous_dma(reason="one value a partition"):
+            nc.sync.dma_start(out=cal[:, 0:2], in_=so.rearrange("(c p) o -> p (c o)", p=P))
+            nc.sync.dma_start(out=cal[:, 8:10], in_=bo.rearrange("(c p) o -> p (c o)", p=P))
+
+        hid_q = sb("hid_q", [P, J], U32)
+        hid_s = sb("hid_s", [P, J], U8)
+        accs = [psum.tile([P, 4, HALF], F32, name="acc%d" % h) for h in range(2)]
+        for i, fmt in enumerate((E5M2, E4M3)):
+            for h in range(2):
+                cols = slice(h * HALF, (h + 1) * HALF)
+                for t in range(4):
+                    nc.tensor.matmul_mx(
+                        out=accs[h][:, t, :],
+                        lhsT=w_dealt[i][:, 256 * t : 256 * (t + 1)].bitcast(E2M1),
+                        lhsT_scale=planes1[i][:, J + P * t : J + P * (t + 1)],
+                        rhs=x_g[i][:, cols].bitcast(fmt),
+                        rhs_scale=planes1[i][:, cols],
+                        start=(i == 0 and t == 0), stop=(i == 1 and t == 3),
+                    )
+
+        m_ps = psum.tile([P, 2, J], F32, name="m_ps")
+        p_ps = psum.tile([P, 2, J], F32, name="p_ps")
+        q_ps = psum.tile([P, 2, J], F32, name="q_ps")
+        for h in range(2):
+            cols = slice(h * HALF, (h + 1) * HALF)
+            hid = sb("hid%d" % h, [P, HALF, 4], BF16)
+            if h == 1:
+                nc.scalar.activation(out=hid[:], in_=accs[h][:].rearrange("p t j -> p j t"), func=ACT.Relu)
+            else:
+                nc.vector.tensor_scalar_max(hid[:], accs[h][:].rearrange("p t j -> p j t"), 0.0)
+            nc.vector.quantize_mx(
+                out=hid_q[:, cols].bitcast(E4M3), scales=hid_s[:, cols], in_=hid[:].rearrange("p j t -> p (j t)")
+            )
+            for i, (ps, fmt) in enumerate(((m_ps, E5M2), (p_ps, E2M1), (q_ps, E4M3))):
+                for c in range(2):
+                    if i == 1:
+                        lhsT = wb_sb[:, 256 * c : 256 * (c + 1)]
+                    else:
+                        lhsT = (wd_sb if i == 0 else wc_sb)[:, P * c : P * (c + 1)]
+                    nc.tensor.matmul_mx(
+                        out=ps[:, c, cols],
+                        lhsT=lhsT.bitcast(fmt),
+                        lhsT_scale=planes2[:, i * N + P * c : i * N + P * (c + 1)],
+                        rhs=hid_q[:, cols].bitcast(E4M3),
+                        rhs_scale=hid_s[:, cols],
+                        start=True, stop=True,
+                    )
+
+        m_sb = [sb("m_sb%d" % c, [P, J], F32) for c in range(2)]
+        p_sb = sb("p_sb", [P, 2 * J], F32)
+        q_sb = sb("q_sb", [P, 2 * J], F32)
+        for c in range(2):
+            nc.scalar.copy(m_sb[c][:], m_ps[:, c, :])
+        nc.vector.tensor_copy(p_sb[:], p_ps[:].rearrange("p c j -> p (c j)"))
+        nc.scalar.copy(q_sb[:], q_ps[:].rearrange("p c j -> p (c j)"))
+        gate = [sb("gate%d" % c, [P, O], F32) for c in range(2)]
+        pg = [sb("pg%d" % c, [P, O], F32) for c in range(2)]
+        qg = [sb("qg%d" % c, [P, O], F32) for c in range(2)]
+        for c in range(2):
+            nc.scalar.activation(
+                out=gate[c][:], in_=m_sb[c][:].indirect(l5[:]), func=ACT.Sigmoid,
+                bias=cal[:, 8 + c : 9 + c], scale=cal[:, c : c + 1],
+            )
+            nc.vector.tensor_copy(pg[c][:], p_sb[:, c * J : (c + 1) * J].indirect(l3[:]))
+        nc.vector.tensor_copy(qg[0][:], q_sb[:, 0:J].indirect(l4[:]))
+        nc.scalar.activation(out=qg[1][:], in_=q_sb[:, J : 2 * J].indirect(l4[:]), func=ACT.Copy)
+        for c in range(2):
+            big = sb("big%d" % c, [P, O], F32)
+            res = sb("res%d" % c, [P, O], F32)
+            nc.vector.tensor_tensor(big[:], pg[c][:], qg[c][:], ALU.max)
+            nc.vector.tensor_tensor(res[:], big[:], gate[c][:], ALU.mult)
+            (nc.scalar if c == 0 else nc.sync).dma_start(out=out[c * P : (c + 1) * P, :], in_=res[:])

@@ -49,6 +49,11 @@ def tile_list_threeoutcomes_bank_kernel(
                     in_=planes[8 * r : P : 32, :].bitcast(I32),
                 )
 
+        warm_in = sb("warm_in", [P, 1], F32)
+        warm_out = sb("warm_out", [P, 1], F32)
+        nc.vector.memset(warm_in[:], 0.0)
+        nc.scalar.activation(out=warm_out[:], in_=warm_in[:], func=ACT.Sigmoid)
+
         xt_tab = sb("xt_tab", [P, T], I32)
         xo_tab = sb("xo_tab", [P, T], I32)
         planes2 = sb("planes2", [P, 3 * N], U8)

@@ -18,8 +18,16 @@ ACT = mybir.ActivationFunctionType
 ALU = mybir.AluOpType
 
 P = 128
-ROWS = 16
-HALF = 128
+PACK = 4
+BLOCKS = 16
+QUADS = 4
+QUAD = P // QUADS
+LIVE = BLOCKS // QUADS
+HALF = J // 2
+TILES = N // P
+GROUP = 16
+FP4_BYTES = 2
+BIAS_COL = 8
 
 
 def tile_list_threeoutcomes_bank_kernel(
@@ -32,164 +40,194 @@ def tile_list_threeoutcomes_bank_kernel(
         pool = ctx.enter_context(tc.tile_pool(name="sbuf", bufs=1))
         psum = ctx.enter_context(tc.psum_pool(name="psum", bufs=1))
 
-        def sb(name, shape, dtype, tag=""):
-            return pool.tile(shape, dtype, name=name, tag=tag or name, align_bytes=64)
+        def sb(name, shape, dtype, reuse=""):
+            return pool.tile(shape, dtype, name=name, tag=reuse or name, align_bytes=64)
 
-        def words(ap):
+        def fp8_words(ap):
             return ap[0].rearrange("p n t -> p (n t)").bitcast(I32)
 
-        def per_block(scales):
+        def rows_in_pairs(scales):
             rows = scales[0].bitcast(I32)
-            return rows.unsqueeze(1).broadcast_to([ROWS, 8, rows.shape[1]])
-
-        def gather_rows(planes):
-            for r in range(1, 4):
-                nc.sync.dma_start(
-                    out=planes[r:P:32, :].bitcast(I32),
-                    in_=planes[8 * r : P : 32, :].bitcast(I32),
-                )
+            return rows.unsqueeze(1).broadcast_to([BLOCKS, 2, rows.shape[1]])
 
         warm_in = sb("warm_in", [P, 1], F32)
         warm_out = sb("warm_out", [P, 1], F32)
         nc.vector.memset(warm_in[:], 0.0)
         nc.scalar.activation(out=warm_out[:], in_=warm_in[:], func=ACT.Sigmoid)
 
-        xt_tab = sb("xt_tab", [P, T], I32)
-        xo_tab = sb("xo_tab", [P, T], I32)
-        planes2 = sb("planes2", [P, 3 * N], U8)
-        nc.gpsimd.dma_start(out=xt_tab[:], in_=words(xt_words))
-        nc.gpsimd.dma_start(out=xo_tab[:], in_=words(xo_words))
-        for i, sc in enumerate((wd_scales, wb_scales, wc_scales)):
-            nc.gpsimd.dma_start(out=planes2[:, i * N : (i + 1) * N].bitcast(I32), in_=per_block(sc))
-
-        l1 = sb("l1", [P, J // 16], U16)
-        l2 = sb("l2", [P, J // 16], U16)
-        l3 = sb("l3", [P, O // 16], U16)
-        l4 = sb("l4", [P, O // 16], U16)
-        l5 = sb("l5", [P, O // 16], U16)
+        xt_table = sb("xt_table", [P, T], I32)
+        xo_table = sb("xo_table", [P, T], I32)
         xt_rows = sb("xt_rows", [P, T], U8)
         xo_rows = sb("xo_rows", [P, T], U8)
-        w_rows = sb("w_rows", [P, R], U8)
-        w0_rows = sb("w0_rows", [P, R], U8)
-        w_raw = sb("w_raw", [P, 2 * R], U8)
-        w0_raw = sb("w0_raw", [P, 2 * R], U8)
-        nc.sync.dma_start(out=xt_rows[:].bitcast(I32), in_=per_block(xt_scales))
-        nc.sync.dma_start(l1[:], offs)
-        nc.sync.dma_start(out=w_rows[:].bitcast(I32), in_=per_block(w_scales))
-        nc.sync.dma_start(out=xo_rows[:].bitcast(I32), in_=per_block(xo_scales))
-        nc.sync.dma_start(l2[:], offs2)
-        nc.sync.dma_start(out=w0_rows[:].bitcast(I32), in_=per_block(w0_scales))
+        w_rows = sb("w_rows", [P, 2 * R], U8)
+        set_widths = (J + R, J + R + 2 * N)
+        planes = [sb("planes%d" % s, [P, set_widths[s]], U8) for s in range(2)]
+        staged = [sb("staged%d" % s, [P, set_widths[s]], U8) for s in range(2)]
+        wb_plane = planes[1][:, J + R : J + R + N]
+        wc_plane = planes[1][:, J + R + N :]
+        wd_plane = staged[1][:, J : J + N]
+        for rows in (xt_rows, w_rows, xo_rows):
+            nc.vector.memset(rows[QUAD : 2 * QUAD, :].bitcast(I32), 0)
+            nc.vector.memset(rows[2 * QUAD : P, :].bitcast(I32), 0)
+        for plane_set in planes:
+            nc.vector.memset(plane_set[:].bitcast(I32), 0)
+
+        nc.gpsimd.dma_start(out=xt_table[:], in_=fp8_words(xt_words))
+        nc.gpsimd.dma_start(out=xo_table[:], in_=fp8_words(xo_words))
+
+        xt_list = sb("xt_list", [P, J // GROUP], U16)
+        xo_list = sb("xo_list", [P, J // GROUP], U16)
+        p_list = sb("p_list", [P, O // GROUP], U16)
+        q_list = sb("q_list", [P, O // GROUP], U16)
+        m_list = sb("m_list", [P, O // GROUP], U16)
+        w_raw = sb("w_raw", [P, FP4_BYTES * R], U8)
+        nc.sync.dma_start(out=xt_rows[0:QUAD, :].bitcast(I32), in_=rows_in_pairs(xt_scales))
+        nc.sync.dma_start(xt_list[:], offs)
+        nc.sync.dma_start(out=w_rows[0:QUAD, 0:R].bitcast(I32), in_=rows_in_pairs(w_scales))
+        nc.sync.dma_start(out=xo_rows[0:QUAD, :].bitcast(I32), in_=rows_in_pairs(xo_scales))
+        nc.sync.dma_start(xo_list[:], offs2)
+        nc.sync.dma_start(out=w_rows[0:QUAD, R:].bitcast(I32), in_=rows_in_pairs(w0_scales))
         nc.sync.dma_start(out=w_raw[:].bitcast(I32), in_=w_words[0].bitcast(I32))
+        for i, scales in enumerate((wb_scales, wc_scales)):
+            first = J + R + i * N
+            nc.sync.dma_start(out=staged[1][0:QUAD:2, first : first + N].bitcast(I32), in_=scales[0].bitcast(I32))
+        nc.sync.dma_start(m_list[:], offs5)
+        nc.sync.dma_start(p_list[:], offs3)
+        nc.sync.dma_start(q_list[:], offs4)
+
+        def make_planes(s, x_rows, x_list):
+            picked = sb("picked%d" % s, [P, J], U8)
+            nc.vector.tensor_copy(picked[:], x_rows[:].indirect(x_list[:]))
+            nc.vector.tensor_copy(
+                staged[s][:, J : J + R].rearrange("p (t m) -> p t m", t=PACK),
+                w_rows[:, s * R : (s + 1) * R].rearrange("p (m t) -> p t m", t=PACK),
+            )
+            nc.vector.tensor_copy(staged[s][:, 0:J].bitcast(I32), picked[:].bitcast(I32))
+            for quad in range(QUADS):
+                nc.sync.dma_start(
+                    out=planes[s][QUAD * quad : QUAD * quad + LIVE, :].bitcast(I32),
+                    in_=staged[s][2 * LIVE * quad : 2 * LIVE * (quad + 1) : 2, :].bitcast(I32),
+                )
+
+        make_planes(0, xt_rows, xt_list)
+        w0_raw = sb("w0_raw", [P, FP4_BYTES * R], U8, reuse="picked0")
         nc.sync.dma_start(out=w0_raw[:].bitcast(I32), in_=w0_words[0].bitcast(I32))
-        nc.sync.dma_start(l5[:], offs5)
-        nc.sync.dma_start(l3[:], offs3)
-        nc.sync.dma_start(l4[:], offs4)
+        make_planes(1, xo_rows, xo_list)
 
-        planes1 = []
-        for i, (x_rows, lst, wt_rows) in enumerate(((xt_rows, l1, w_rows), (xo_rows, l2, w0_rows))):
-            picked = sb("picked%d" % i, [P, J], U8)
-            planes = sb("planes1_%d" % i, [P, J + R], U8)
-            nc.vector.tensor_copy(picked[:], x_rows[:].indirect(lst[:]))
+        def make_words(s, table, x_list, raw, picked_reuse, dealt_reuse):
+            picked = sb("x_words%d" % s, [P, J], U32, reuse=picked_reuse)
+            dealt = sb("w_dealt%d" % s, [P, FP4_BYTES * R], U8, reuse=dealt_reuse)
+            nc.vector.tensor_copy(picked[:], table[:].bitcast(U32).indirect(x_list[:]))
             nc.vector.tensor_copy(
-                planes[:, J:].rearrange("p (t m) -> p t m", t=4),
-                wt_rows[:].rearrange("p (m t) -> p t m", t=4),
+                dealt[:].bitcast(U16).rearrange("p (t m) -> p t m", t=PACK),
+                raw[:].bitcast(U16).rearrange("p (m t) -> p t m", t=PACK),
             )
-            nc.vector.tensor_copy(planes[:, 0:J].bitcast(I32), picked[:].bitcast(I32))
-            gather_rows(planes)
-            planes1.append(planes)
+            return picked, dealt
 
-        x_g = []
-        w_dealt = []
-        for i, (tab, lst, raw) in enumerate(((xt_tab, l1, w_raw), (xo_tab, l2, w0_raw))):
-            g = sb("x_g%d" % i, [P, J], U32)
-            dealt = sb("w_dealt%d" % i, [P, 2 * R], U8)
-            nc.vector.tensor_copy(g[:], tab[:].bitcast(U32).indirect(lst[:]))
-            nc.vector.tensor_copy(
-                dealt[:].bitcast(U16).rearrange("p (t m) -> p t m", t=4),
-                raw[:].bitcast(U16).rearrange("p (m t) -> p t m", t=4),
+        first_operands = [
+            make_words(0, xt_table, xt_list, w_raw, "picked1", "w_rows"),
+            make_words(1, xo_table, xo_list, w0_raw, "w_raw", "xo_table"),
+        ]
+
+        out_words = sb("out_words", [P, (PACK + FP4_BYTES + PACK) * N], U8, reuse="xt_table")
+        wd_codes = out_words[:, 0 : PACK * N].bitcast(I32)
+        wb_codes = out_words[:, PACK * N : (PACK + FP4_BYTES) * N]
+        wc_codes = out_words[:, (PACK + FP4_BYTES) * N :].bitcast(I32)
+        nc.sync.dma_start(out=wb_codes.bitcast(I32), in_=wb_words[0].bitcast(I32))
+        nc.sync.dma_start(out=wc_codes, in_=fp8_words(wc_words))
+        nc.sync.dma_start(out=wd_codes, in_=fp8_words(wd_words))
+        for quad in range(QUADS):
+            nc.sync.dma_start(
+                out=wd_plane[QUAD * quad : QUAD * quad + LIVE, :].bitcast(I32),
+                in_=wd_scales[0][LIVE * quad : LIVE * (quad + 1), :].bitcast(I32),
             )
-            x_g.append(g)
-            w_dealt.append(dealt)
 
-        w2 = sb("w2", [P, 10 * N], U8, tag="xt_tab")
-        wd_sb = w2[:, 0 : 4 * N].bitcast(I32)
-        wb_sb = w2[:, 4 * N : 6 * N]
-        wc_sb = w2[:, 6 * N : 10 * N].bitcast(I32)
-        nc.sync.dma_start(out=wd_sb, in_=words(wd_words))
-        nc.sync.dma_start(out=wb_sb.bitcast(I32), in_=wb_words[0].bitcast(I32))
-        nc.sync.dma_start(out=wc_sb, in_=words(wc_words))
-        gather_rows(planes2)
+        calib = sb("calib", [P, 2 * BIAS_COL], F32, reuse="picked0")
+        with nc.allow_non_contiguous_dma(reason="one value a partition and row tile"):
+            nc.sync.dma_start(out=calib[:, 0:TILES], in_=so.rearrange("(c p) o -> p (c o)", p=P))
+            nc.sync.dma_start(out=calib[:, BIAS_COL : BIAS_COL + TILES], in_=bo.rearrange("(c p) o -> p (c o)", p=P))
 
-        cal = sb("cal", [P, 16], F32, tag="xo_tab")
-        with nc.allow_non_contiguous_dma(reason="one value a partition"):
-            nc.sync.dma_start(out=cal[:, 0:2], in_=so.rearrange("(c p) o -> p (c o)", p=P))
-            nc.sync.dma_start(out=cal[:, 8:10], in_=bo.rearrange("(c p) o -> p (c o)", p=P))
-
-        hid_q = sb("hid_q", [P, J], U32)
-        hid_s = sb("hid_s", [P, J], U8)
-        accs = [psum.tile([P, 4, HALF], F32, name="acc%d" % h) for h in range(2)]
-        for i, fmt in enumerate((E5M2, E4M3)):
+        hid_codes = sb("hid_codes", [P, J], U32)
+        hid_plane = sb("hid_plane", [P, J], U8)
+        a_ps = [psum.tile([P, PACK, HALF], F32, name="a_ps%d" % h) for h in range(2)]
+        for s, x_format in enumerate((E5M2, E4M3)):
+            x_codes, w_dealt = first_operands[s]
             for h in range(2):
-                cols = slice(h * HALF, (h + 1) * HALF)
-                for t in range(4):
+                slots = slice(h * HALF, (h + 1) * HALF)
+                for t in range(PACK):
                     nc.tensor.matmul_mx(
-                        out=accs[h][:, t, :],
-                        lhsT=w_dealt[i][:, 256 * t : 256 * (t + 1)].bitcast(E2M1),
-                        lhsT_scale=planes1[i][:, J + P * t : J + P * (t + 1)],
-                        rhs=x_g[i][:, cols].bitcast(fmt),
-                        rhs_scale=planes1[i][:, cols],
-                        start=(i == 0 and t == 0), stop=(i == 1 and t == 3),
+                        out=a_ps[h][:, t, :],
+                        lhsT=w_dealt[:, FP4_BYTES * P * t : FP4_BYTES * P * (t + 1)].bitcast(E2M1),
+                        lhsT_scale=planes[s][:, J + P * t : J + P * (t + 1)],
+                        rhs=x_codes[:, slots].bitcast(x_format),
+                        rhs_scale=planes[s][:, slots],
+                        start=(s == 0 and t == 0), stop=(s == 1 and t == PACK - 1),
                     )
 
-        m_ps = psum.tile([P, 2, J], F32, name="m_ps")
-        p_ps = psum.tile([P, 2, J], F32, name="p_ps")
-        q_ps = psum.tile([P, 2, J], F32, name="q_ps")
-        for h in range(2):
-            cols = slice(h * HALF, (h + 1) * HALF)
-            hid = sb("hid%d" % h, [P, HALF, 4], BF16)
-            if h == 1:
-                nc.scalar.activation(out=hid[:], in_=accs[h][:].rearrange("p t j -> p j t"), func=ACT.Relu)
-            else:
-                nc.vector.tensor_scalar_max(hid[:], accs[h][:].rearrange("p t j -> p j t"), 0.0)
+        pq_ps = [[psum.tile([P, 2, HALF], F32, name="pq_ps%d%d" % (h, c)) for c in range(TILES)] for h in range(2)]
+        m_ps = [psum.tile([P, J], F32, name="m_ps%d" % c) for c in range(TILES)]
+        pq_weights = ((wb_codes, FP4_BYTES * P, E2M1, wb_plane), (wc_codes, P, E4M3, wc_plane))
+
+        def quantise_and_multiply(h, hid):
+            slots = slice(h * HALF, (h + 1) * HALF)
             nc.vector.quantize_mx(
-                out=hid_q[:, cols].bitcast(E4M3), scales=hid_s[:, cols], in_=hid[:].rearrange("p j t -> p (j t)")
+                out=hid_codes[:, slots].bitcast(E4M3),
+                scales=hid_plane[:, slots],
+                in_=hid[:].rearrange("p j t -> p (j t)"),
             )
-            for i, (ps, fmt) in enumerate(((m_ps, E5M2), (p_ps, E2M1), (q_ps, E4M3))):
-                for c in range(2):
-                    if i == 1:
-                        lhsT = wb_sb[:, 256 * c : 256 * (c + 1)]
-                    else:
-                        lhsT = (wd_sb if i == 0 else wc_sb)[:, P * c : P * (c + 1)]
+            for c in range(TILES):
+                for i, (codes, width, w_format, w_plane) in enumerate(pq_weights):
                     nc.tensor.matmul_mx(
-                        out=ps[:, c, cols],
-                        lhsT=lhsT.bitcast(fmt),
-                        lhsT_scale=planes2[:, i * N + P * c : i * N + P * (c + 1)],
-                        rhs=hid_q[:, cols].bitcast(E4M3),
-                        rhs_scale=hid_s[:, cols],
+                        out=pq_ps[h][c][:, i, :],
+                        lhsT=codes[:, width * c : width * (c + 1)].bitcast(w_format),
+                        lhsT_scale=w_plane[:, P * c : P * (c + 1)],
+                        rhs=hid_codes[:, slots].bitcast(E4M3),
+                        rhs_scale=hid_plane[:, slots],
                         start=True, stop=True,
                     )
 
-        m_sb = [sb("m_sb%d" % c, [P, J], F32) for c in range(2)]
-        p_sb = sb("p_sb", [P, 2 * J], F32)
-        q_sb = sb("q_sb", [P, 2 * J], F32)
-        for c in range(2):
-            nc.scalar.copy(m_sb[c][:], m_ps[:, c, :])
-        nc.vector.tensor_copy(p_sb[:], p_ps[:].rearrange("p c j -> p (c j)"))
-        nc.scalar.copy(q_sb[:], q_ps[:].rearrange("p c j -> p (c j)"))
-        gate = [sb("gate%d" % c, [P, O], F32) for c in range(2)]
-        pg = [sb("pg%d" % c, [P, O], F32) for c in range(2)]
-        qg = [sb("qg%d" % c, [P, O], F32) for c in range(2)]
-        for c in range(2):
-            nc.scalar.activation(
-                out=gate[c][:], in_=m_sb[c][:].indirect(l5[:]), func=ACT.Sigmoid,
-                bias=cal[:, 8 + c : 9 + c], scale=cal[:, c : c + 1],
+        hid_first = sb("hid_first", [P, HALF, PACK], BF16)
+        nc.vector.tensor_scalar_max(hid_first[:], a_ps[0][:].rearrange("p t j -> p j t"), 0.0)
+        quantise_and_multiply(0, hid_first)
+        hid_second = sb("hid_second", [P, HALF, PACK], BF16)
+        nc.scalar.activation(out=hid_second[:], in_=a_ps[1][:].rearrange("p t j -> p j t"), func=ACT.Relu)
+        quantise_and_multiply(1, hid_second)
+        for c in range(TILES):
+            nc.tensor.matmul_mx(
+                out=m_ps[c][:],
+                lhsT=wd_codes[:, P * c : P * (c + 1)].bitcast(E5M2),
+                lhsT_scale=wd_plane[:, P * c : P * (c + 1)],
+                rhs=hid_codes[:].bitcast(E4M3),
+                rhs_scale=hid_plane[:],
+                start=True, stop=True,
             )
-            nc.vector.tensor_copy(pg[c][:], p_sb[:, c * J : (c + 1) * J].indirect(l3[:]))
-        nc.vector.tensor_copy(qg[0][:], q_sb[:, 0:J].indirect(l4[:]))
-        nc.scalar.activation(out=qg[1][:], in_=q_sb[:, J : 2 * J].indirect(l4[:]), func=ACT.Copy)
-        for c in range(2):
-            big = sb("big%d" % c, [P, O], F32)
-            res = sb("res%d" % c, [P, O], F32)
-            nc.vector.tensor_tensor(big[:], pg[c][:], qg[c][:], ALU.max)
-            nc.vector.tensor_tensor(res[:], big[:], gate[c][:], ALU.mult)
-            (nc.scalar if c == 0 else nc.sync).dma_start(out=out[c * P : (c + 1) * P, :], in_=res[:])
+
+        m0 = [sb("m0_%d" % c, [P, J], F32) for c in range(TILES)]
+        pq = [sb("pq%d" % c, [P, 2, J], F32) for c in range(TILES)]
+        for h in range(2):
+            slots = slice(h * HALF, (h + 1) * HALF)
+            nc.vector.tensor_copy(pq[0][:, :, slots], pq_ps[h][0][:])
+            nc.scalar.copy(pq[1][:, :, slots], pq_ps[h][1][:])
+        for c in range(TILES):
+            nc.scalar.copy(m0[c][:], m_ps[c][:])
+
+        gate = [sb("gate%d" % c, [P, O], F32) for c in range(TILES)]
+        p_picked = [sb("p_picked%d" % c, [P, O], F32) for c in range(TILES)]
+        q_picked = [sb("q_picked%d" % c, [P, O], F32) for c in range(TILES)]
+        nc.vector.tensor_copy(p_picked[0][:], pq[0][:, 0, :].indirect(p_list[:]))
+        nc.vector.tensor_copy(q_picked[0][:], pq[0][:, 1, :].indirect(q_list[:]))
+        nc.vector.tensor_copy(p_picked[1][:], pq[1][:, 0, :].indirect(p_list[:]))
+        nc.scalar.activation(out=q_picked[1][:], in_=pq[1][:, 1, :].indirect(q_list[:]), func=ACT.Copy)
+        for c in range(TILES):
+            nc.scalar.activation(
+                out=gate[c][:], in_=m0[c][:].indirect(m_list[:]), func=ACT.Sigmoid,
+                bias=calib[:, BIAS_COL + c : BIAS_COL + c + 1], scale=calib[:, c : c + 1],
+            )
+
+        larger = [sb("larger%d" % c, [P, O], F32) for c in range(TILES)]
+        for c in range(TILES):
+            nc.vector.tensor_tensor(larger[c][:], p_picked[c][:], q_picked[c][:], ALU.max)
+        for c, queue in enumerate((nc.scalar, nc.sync)):
+            result = sb("result%d" % c, [P, O], F32)
+            nc.vector.tensor_tensor(result[:], larger[c][:], gate[c][:], ALU.mult)
+            queue.dma_start(out=out[c * P : (c + 1) * P, :], in_=result[:])

from contextlib import ExitStack

import concourse.mybir as mybir

K, T, J, R, N, O = 512, 1024, 256, 512, 256, 128
FLOPS = 2 * 2 * K * R * J + 3 * 2 * R * N * J

F32 = mybir.dt.float32
BF16 = mybir.dt.bfloat16
I32 = mybir.dt.int32
U32 = mybir.dt.uint32
U16 = mybir.dt.uint16
U8 = mybir.dt.uint8
E4M3 = mybir.dt.float8_e4m3fn_x4
E5M2 = mybir.dt.float8_e5m2_x4
E2M1 = mybir.dt.float4_e2m1fn_x4
ACT = mybir.ActivationFunctionType
ALU = mybir.AluOpType

P = 128
PACK = 4
BLOCKS = 16
QUADS = 4
QUAD = P // QUADS
LIVE = BLOCKS // QUADS
HALF = J // 2
TILES = N // P
GROUP = 16
FP4_BYTES = 2
BIAS_COL = 8


def tile_list_threeoutcomes_bank_kernel(
    tc, xt_words, xt_scales, w_words, w_scales, xo_words, xo_scales, w0_words, w0_scales,
    wb_words, wb_scales, wc_words, wc_scales, wd_words, wd_scales, so, bo,
    offs, offs2, offs3, offs4, offs5, out,
):
    nc = tc.nc
    with ExitStack() as ctx:
        pool = ctx.enter_context(tc.tile_pool(name="sbuf", bufs=1))
        psum = ctx.enter_context(tc.psum_pool(name="psum", bufs=1))

        def sb(name, shape, dtype, reuse=""):
            return pool.tile(shape, dtype, name=name, tag=reuse or name, align_bytes=64)

        def fp8_words(ap):
            return ap[0].rearrange("p n t -> p (n t)").bitcast(I32)

        def rows_in_pairs(scales):
            rows = scales[0].bitcast(I32)
            return rows.unsqueeze(1).broadcast_to([BLOCKS, 2, rows.shape[1]])

        warm_in = sb("warm_in", [P, 1], F32)
        warm_out = sb("warm_out", [P, 1], F32)
        nc.vector.memset(warm_in[:], 0.0)
        nc.scalar.activation(out=warm_out[:], in_=warm_in[:], func=ACT.Sigmoid)

        xt_table = sb("xt_table", [P, T], I32)
        xo_table = sb("xo_table", [P, T], I32)
        xt_rows = sb("xt_rows", [P, T], U8)
        xo_rows = sb("xo_rows", [P, T], U8)
        w_rows = sb("w_rows", [P, 2 * R], U8)
        set_widths = (J + R, J + R + 2 * N)
        planes = [sb("planes%d" % s, [P, set_widths[s]], U8) for s in range(2)]
        staged = [sb("staged%d" % s, [P, set_widths[s]], U8) for s in range(2)]
        wb_plane = planes[1][:, J + R : J + R + N]
        wc_plane = planes[1][:, J + R + N :]
        wd_plane = staged[1][:, J : J + N]
        for rows in (xt_rows, w_rows, xo_rows):
            nc.vector.memset(rows[QUAD : 2 * QUAD, :].bitcast(I32), 0)
            nc.vector.memset(rows[2 * QUAD : P, :].bitcast(I32), 0)
        for plane_set in planes:
            nc.vector.memset(plane_set[:].bitcast(I32), 0)

        nc.gpsimd.dma_start(out=xt_table[:], in_=fp8_words(xt_words))
        nc.gpsimd.dma_start(out=xo_table[:], in_=fp8_words(xo_words))

        xt_list = sb("xt_list", [P, J // GROUP], U16)
        xo_list = sb("xo_list", [P, J // GROUP], U16)
        p_list = sb("p_list", [P, O // GROUP], U16)
        q_list = sb("q_list", [P, O // GROUP], U16)
        m_list = sb("m_list", [P, O // GROUP], U16)
        w_raw = sb("w_raw", [P, FP4_BYTES * R], U8)
        nc.sync.dma_start(out=xt_rows[0:QUAD, :].bitcast(I32), in_=rows_in_pairs(xt_scales))
        nc.sync.dma_start(xt_list[:], offs)
        nc.sync.dma_start(out=w_rows[0:QUAD, 0:R].bitcast(I32), in_=rows_in_pairs(w_scales))
        nc.sync.dma_start(out=xo_rows[0:QUAD, :].bitcast(I32), in_=rows_in_pairs(xo_scales))
        nc.sync.dma_start(xo_list[:], offs2)
        nc.sync.dma_start(out=w_rows[0:QUAD, R:].bitcast(I32), in_=rows_in_pairs(w0_scales))
        nc.sync.dma_start(out=w_raw[:].bitcast(I32), in_=w_words[0].bitcast(I32))
        for i, scales in enumerate((wb_scales, wc_scales)):
            first = J + R + i * N
            nc.sync.dma_start(out=staged[1][0:QUAD:2, first : first + N].bitcast(I32), in_=scales[0].bitcast(I32))
        nc.sync.dma_start(m_list[:], offs5)
        nc.sync.dma_start(p_list[:], offs3)
        nc.sync.dma_start(q_list[:], offs4)

        def make_planes(s, x_rows, x_list):
            picked = sb("picked%d" % s, [P, J], U8)
            nc.vector.tensor_copy(picked[:], x_rows[:].indirect(x_list[:]))
            nc.vector.tensor_copy(
                staged[s][:, J : J + R].rearrange("p (t m) -> p t m", t=PACK),
                w_rows[:, s * R : (s + 1) * R].rearrange("p (m t) -> p t m", t=PACK),
            )
            nc.vector.tensor_copy(staged[s][:, 0:J].bitcast(I32), picked[:].bitcast(I32))
            for quad in range(QUADS):
                nc.sync.dma_start(
                    out=planes[s][QUAD * quad : QUAD * quad + LIVE, :].bitcast(I32),
                    in_=staged[s][2 * LIVE * quad : 2 * LIVE * (quad + 1) : 2, :].bitcast(I32),
                )

        make_planes(0, xt_rows, xt_list)
        w0_raw = sb("w0_raw", [P, FP4_BYTES * R], U8, reuse="picked0")
        nc.sync.dma_start(out=w0_raw[:].bitcast(I32), in_=w0_words[0].bitcast(I32))
        make_planes(1, xo_rows, xo_list)

        def make_words(s, table, x_list, raw, picked_reuse, dealt_reuse):
            picked = sb("x_words%d" % s, [P, J], U32, reuse=picked_reuse)
            dealt = sb("w_dealt%d" % s, [P, FP4_BYTES * R], U8, reuse=dealt_reuse)
            nc.vector.tensor_copy(picked[:], table[:].bitcast(U32).indirect(x_list[:]))
            nc.vector.tensor_copy(
                dealt[:].bitcast(U16).rearrange("p (t m) -> p t m", t=PACK),
                raw[:].bitcast(U16).rearrange("p (m t) -> p t m", t=PACK),
            )
            return picked, dealt

        first_operands = [
            make_words(0, xt_table, xt_list, w_raw, "picked1", "w_rows"),
            make_words(1, xo_table, xo_list, w0_raw, "w_raw", "xo_table"),
        ]

        out_words = sb("out_words", [P, (PACK + FP4_BYTES + PACK) * N], U8, reuse="xt_table")
        wd_codes = out_words[:, 0 : PACK * N].bitcast(I32)
        wb_codes = out_words[:, PACK * N : (PACK + FP4_BYTES) * N]
        wc_codes = out_words[:, (PACK + FP4_BYTES) * N :].bitcast(I32)
        nc.sync.dma_start(out=wb_codes.bitcast(I32), in_=wb_words[0].bitcast(I32))
        nc.sync.dma_start(out=wc_codes, in_=fp8_words(wc_words))
        nc.sync.dma_start(out=wd_codes, in_=fp8_words(wd_words))
        for quad in range(QUADS):
            nc.sync.dma_start(
                out=wd_plane[QUAD * quad : QUAD * quad + LIVE, :].bitcast(I32),
                in_=wd_scales[0][LIVE * quad : LIVE * (quad + 1), :].bitcast(I32),
            )

        calib = sb("calib", [P, 2 * BIAS_COL], F32, reuse="picked0")
        with nc.allow_non_contiguous_dma(reason="one value a partition and row tile"):
            nc.sync.dma_start(out=calib[:, 0:TILES], in_=so.rearrange("(c p) o -> p (c o)", p=P))
            nc.sync.dma_start(out=calib[:, BIAS_COL : BIAS_COL + TILES], in_=bo.rearrange("(c p) o -> p (c o)", p=P))

        hid_codes = sb("hid_codes", [P, J], U32)
        hid_plane = sb("hid_plane", [P, J], U8)
        a_ps = [psum.tile([P, PACK, HALF], F32, name="a_ps%d" % h) for h in range(2)]
        for s, x_format in enumerate((E5M2, E4M3)):
            x_codes, w_dealt = first_operands[s]
            for h in range(2):
                slots = slice(h * HALF, (h + 1) * HALF)
                for t in range(PACK):
                    nc.tensor.matmul_mx(
                        out=a_ps[h][:, t, :],
                        lhsT=w_dealt[:, FP4_BYTES * P * t : FP4_BYTES * P * (t + 1)].bitcast(E2M1),
                        lhsT_scale=planes[s][:, J + P * t : J + P * (t + 1)],
                        rhs=x_codes[:, slots].bitcast(x_format),
                        rhs_scale=planes[s][:, slots],
                        start=(s == 0 and t == 0), stop=(s == 1 and t == PACK - 1),
                    )

        pq_ps = [[psum.tile([P, 2, HALF], F32, name="pq_ps%d%d" % (h, c)) for c in range(TILES)] for h in range(2)]
        m_ps = [psum.tile([P, J], F32, name="m_ps%d" % c) for c in range(TILES)]
        pq_weights = ((wb_codes, FP4_BYTES * P, E2M1, wb_plane), (wc_codes, P, E4M3, wc_plane))

        def quantise_and_multiply(h, hid):
            slots = slice(h * HALF, (h + 1) * HALF)
            nc.vector.quantize_mx(
                out=hid_codes[:, slots].bitcast(E4M3),
                scales=hid_plane[:, slots],
                in_=hid[:].rearrange("p j t -> p (j t)"),
            )
            for c in range(TILES):
                for i, (codes, width, w_format, w_plane) in enumerate(pq_weights):
                    nc.tensor.matmul_mx(
                        out=pq_ps[h][c][:, i, :],
                        lhsT=codes[:, width * c : width * (c + 1)].bitcast(w_format),
                        lhsT_scale=w_plane[:, P * c : P * (c + 1)],
                        rhs=hid_codes[:, slots].bitcast(E4M3),
                        rhs_scale=hid_plane[:, slots],
                        start=True, stop=True,
                    )

        hid_first = sb("hid_first", [P, HALF, PACK], BF16)
        nc.vector.tensor_scalar_max(hid_first[:], a_ps[0][:].rearrange("p t j -> p j t"), 0.0)
        quantise_and_multiply(0, hid_first)
        hid_second = sb("hid_second", [P, HALF, PACK], BF16)
        nc.scalar.activation(out=hid_second[:], in_=a_ps[1][:].rearrange("p t j -> p j t"), func=ACT.Relu)
        quantise_and_multiply(1, hid_second)
        for c in range(TILES):
            nc.tensor.matmul_mx(
                out=m_ps[c][:],
                lhsT=wd_codes[:, P * c : P * (c + 1)].bitcast(E5M2),
                lhsT_scale=wd_plane[:, P * c : P * (c + 1)],
                rhs=hid_codes[:].bitcast(E4M3),
                rhs_scale=hid_plane[:],
                start=True, stop=True,
            )

        m0 = [sb("m0_%d" % c, [P, J], F32) for c in range(TILES)]
        pq = [sb("pq%d" % c, [P, 2, J], F32) for c in range(TILES)]
        for h in range(2):
            slots = slice(h * HALF, (h + 1) * HALF)
            nc.vector.tensor_copy(pq[0][:, :, slots], pq_ps[h][0][:])
            nc.scalar.copy(pq[1][:, :, slots], pq_ps[h][1][:])
        for c in range(TILES):
            nc.scalar.copy(m0[c][:], m_ps[c][:])

        gate = [sb("gate%d" % c, [P, O], F32) for c in range(TILES)]
        p_picked = [sb("p_picked%d" % c, [P, O], F32) for c in range(TILES)]
        q_picked = [sb("q_picked%d" % c, [P, O], F32) for c in range(TILES)]
        nc.vector.tensor_copy(p_picked[0][:], pq[0][:, 0, :].indirect(p_list[:]))
        nc.vector.tensor_copy(q_picked[0][:], pq[0][:, 1, :].indirect(q_list[:]))
        nc.vector.tensor_copy(p_picked[1][:], pq[1][:, 0, :].indirect(p_list[:]))
        nc.scalar.activation(out=q_picked[1][:], in_=pq[1][:, 1, :].indirect(q_list[:]), func=ACT.Copy)
        for c in range(TILES):
            nc.scalar.activation(
                out=gate[c][:], in_=m0[c][:].indirect(m_list[:]), func=ACT.Sigmoid,
                bias=calib[:, BIAS_COL + c : BIAS_COL + c + 1], scale=calib[:, c : c + 1],
            )

        larger = [sb("larger%d" % c, [P, O], F32) for c in range(TILES)]
        for c in range(TILES):
            nc.vector.tensor_tensor(larger[c][:], p_picked[c][:], q_picked[c][:], ALU.max)
        for c, queue in enumerate((nc.scalar, nc.sync)):
            result = sb("result%d" % c, [P, O], F32)
            nc.vector.tensor_tensor(result[:], larger[c][:], gate[c][:], ALU.mult)
            queue.dma_start(out=out[c * P : (c + 1) * P, :], in_=result[:])
